import numpy as np
import ml_dtypes


def mxq(x, axis, fmt="e4m3"):
    dtype, down = {"e4m3": (ml_dtypes.float8_e4m3fn, 7), "e5m2": (ml_dtypes.float8_e5m2, 14)}[fmt]
    v = np.moveaxis(np.asarray(x, np.float32).astype(ml_dtypes.bfloat16).astype(np.float64), axis, -1)
    blocks = v.reshape(v.shape[:-1] + (-1, 32))
    amax = np.abs(blocks).max(-1, keepdims=True)
    byte = np.maximum(np.where(amax > 0, np.frexp(amax)[1] - 1 + 127, 0) - down, 1)
    scale = np.exp2(byte - 127.0)
    codes = (blocks / scale).astype(np.float32).astype(dtype).astype(np.float64)
    return np.moveaxis((codes * scale).reshape(v.shape), -1, axis)


WIDE = False


def mx_kscale(k):
    if not WIDE:
        return np.ones(k)
    levels = np.array([10, -10, 5, -5, 0])
    if k % 512:
        return np.exp2(np.random.permutation(np.resize(levels, k // 32))).repeat(32)
    a = np.empty((k // 512, 16))
    for p in range(k // 512):
        a[p, :8] = np.random.permutation(np.resize(levels, 8))
        for g in range(8):
            far = levels[np.abs(levels - a[p, g]) >= 10]
            a[p, g + 8] = far[np.random.randint(len(far))]
    return np.exp2(a.ravel()).repeat(32)


def f64(x):
    return np.asarray(x).astype(np.float64)


def striped(idx):
    return np.tile(np.asarray(idx).reshape(-1, 16).T, (8, 1)).astype(np.uint16)


def unstriped(offs):
    return offs[:16].T.reshape(-1).astype(np.int64)


def striped8(idx):
    return np.asarray(idx).reshape(8, -1, 16).transpose(0, 2, 1).reshape(128, -1).astype(np.uint16)


def unstriped8(offs):
    return offs.reshape(8, 16, -1).transpose(0, 2, 1).reshape(8, -1).astype(np.int64)


def pick8(x, idx, run):
    r = np.arange(len(x))
    return x[r[:, None], idx[r % (8 * run) // run]]


E2M1 = np.array([0.0, 0.5, 1.0, 1.5, 2.0, 3.0, 4.0, 6.0, -0.0, -0.5, -1.0, -1.5, -2.0, -3.0, -4.0, -6.0])


def pack_weight(w, fmt):
    k, n = w.shape
    w = f64(np.asarray(w, np.float32).astype(ml_dtypes.bfloat16)).reshape(k // 32, 32, n)
    amax = np.abs(w).max(1)
    if fmt == "e4m3":
        byte = np.frexp(amax)[1] - 1 + 127 - 7
    else:
        mant, ex = np.frexp(amax / 6.0)
        byte = np.where(mant > 0.5, ex, ex - 1) + 127
    byte = np.clip(np.where(amax > 0, byte, 1), 1, 254)
    scaled = (w * np.exp2(127.0 - byte)[:, None, :]).reshape(k, n).astype(np.float32)
    by_word = np.ascontiguousarray(scaled.reshape(k // 512, 128, 4, n).transpose(0, 1, 3, 2))
    if fmt == "e4m3":
        words = by_word.astype(ml_dtypes.float8_e4m3fn).view(np.uint8)
    else:
        c = by_word.astype(ml_dtypes.float4_e2m1fn).view(np.uint8) & 0xF
        words = (c[..., 0::2] | (c[..., 1::2] << 4)).reshape(k // 512, 128, 2 * n)
    return np.ascontiguousarray(words), np.ascontiguousarray(byte.astype(np.uint8).reshape(k // 512, 16, n))


def unpack_weight(words, scales, fmt):
    g, _, n = scales.shape
    words = np.ascontiguousarray(words).reshape(g, 128, n, -1)
    if fmt == "e4m3":
        vals = words.view(ml_dtypes.float8_e4m3fn).astype(np.float64)
    else:
        nib = np.empty((g, 128, n, 4), np.uint8)
        nib[..., 0::2] = words & 0xF
        nib[..., 1::2] = words >> 4
        vals = E2M1[nib]
    vals = vals * np.repeat(np.exp2(scales.astype(np.float64) - 127.0), 8, axis=1)[..., None]
    return vals.transpose(0, 1, 3, 2).reshape(g * 512, n)


K, J, R, T, Z, M, O, N, U, E = 512, 512, 512, 2048, 512, 1024, 256, 256, 512, 128


def setup_inputs():
    n = np.random.standard_normal
    idx = np.random.permutation(T)[:J]
    idx2 = np.random.permutation(M)[:J]
    idx3 = np.stack([np.random.permutation(J)[:O] for _ in range(8)])
    idx4 = np.stack([np.random.permutation(U)[:O] for _ in range(8)])
    idx5 = np.stack([np.random.permutation(U)[:O] for _ in range(8)])
    idx6 = np.stack([np.random.permutation(U)[:E] for _ in range(8)])
    idx7 = np.stack([np.random.permutation(U)[:E] for _ in range(8)])
    fk = mx_kscale(K)
    fr = mx_kscale(R)
    fz = mx_kscale(Z)
    xtp = pack_weight(n((K, T)) * fk[:, None], "e2m1")
    wp = pack_weight(n((K, R)) * 1 / np.sqrt(K) / fk[:, None] * fr, "e4m3")
    xop = pack_weight(n((Z, M)) / fz[:, None], "e4m3")
    w2p = pack_weight(n((Z, R)) * 1 / np.sqrt(Z) * fz[:, None] * fr, "e2m1")
    wbp = pack_weight(n((R, N)) * 1 / np.sqrt(R) / fr[:, None], "e2m1")
    wop = pack_weight(n((R, N)) * 1 / np.sqrt(R) / fr[:, None], "e4m3")
    return {
        "xt_words": xtp[0],
        "xt_scales": xtp[1],
        "w_words": wp[0],
        "w_scales": wp[1],
        "xo_words": xop[0],
        "xo_scales": xop[1],
        "w2_words": w2p[0],
        "w2_scales": w2p[1],
        "sa": (np.random.uniform(0.5, 1.6, (R, 1))).astype(np.float32),
        "wb_words": wbp[0],
        "wb_scales": wbp[1],
        "wo_words": wop[0],
        "wo_scales": wop[1],
        "se": (np.random.uniform(0.5, 1.6, (N, 1))).astype(np.float32),
        "sf": (np.random.uniform(0.5, 1.6, (N, 1))).astype(np.float32),
        "offs": striped(idx),
        "offs2": striped(idx2),
        "offs3": striped8(idx3),
        "offs4": striped8(idx4),
        "offs5": striped8(idx5),
        "offs6": striped8(idx6),
        "offs7": striped8(idx7),
    }


def reference(xt_words, xt_scales, w_words, w_scales, xo_words, xo_scales, w2_words, w2_scales, sa, wb_words, wb_scales, wo_words, wo_scales, se, sf, offs, offs2, offs3, offs4, offs5, offs6, offs7):
    idx = unstriped(offs)
    idx2 = unstriped(offs2)
    idx3 = unstriped8(offs3)
    idx4 = unstriped8(offs4)
    idx5 = unstriped8(offs5)
    idx6 = unstriped8(offs6)
    idx7 = unstriped8(offs7)
    xtu = unpack_weight(xt_words, xt_scales, "e2m1")
    wu = unpack_weight(w_words, w_scales, "e4m3")
    xou = unpack_weight(xo_words, xo_scales, "e4m3")
    w2u = unpack_weight(w2_words, w2_scales, "e2m1")
    wbu = unpack_weight(wb_words, wb_scales, "e2m1")
    wou = unpack_weight(wo_words, wo_scales, "e4m3")
    xtidxg = xtu[:, idx]
    xoidx2g = xou[:, idx2]
    a = wu.T @ xtidxg + w2u.T @ xoidx2g
    g1 = np.maximum(a, 0.0)
    hid = pick8(g1, idx3, 64) * f64(sa)
    hidq = mxq(hid, 0, "e4m3")
    p = wbu.T @ hidq
    q = wou.T @ hidq
    m0 = np.zeros((N, U))
    m0[np.arange(N)[:, None], idx4[np.arange(N) % 128 // 16]] = p
    m1 = np.zeros((N, U))
    m1[np.arange(N)[:, None], idx5[np.arange(N) % 128 // 16]] = q
    m2 = np.maximum(m0, m1)
    y = pick8(m2, idx6, 16) * f64(se) - pick8(m1, idx7, 16) * f64(sf)
    return y

@@ -1,0 +1,191 @@
+from contextlib import ExitStack
+
+import concourse.mybir as mybir
+
+F32 = mybir.dt.float32
+BF16 = mybir.dt.bfloat16
+I32 = mybir.dt.int32
+U32 = mybir.dt.uint32
+U16 = mybir.dt.uint16
+U8 = mybir.dt.uint8
+FP8X4 = mybir.dt.float8_e4m3fn_x4
+FP4X4 = mybir.dt.float4_e2m1fn_x4
+ACT = mybir.ActivationFunctionType
+ALU = mybir.AluOpType
+
+K, J, R, T, Z, M, O, N, U, E = 512, 512, 512, 2048, 512, 1024, 256, 256, 512, 128
+P = 128
+PACK = 4
+PER_COLUMN = 16
+HALVES = 2
+FLOPS = 2 * (K * R * J + Z * R * J + 2 * R * N * O)
+
+
+def tile_picked_tokens_plain_bank_kept_outcomes_endreads_kernel(
+    tc, xt_words, xt_scales, w_words, w_scales, xo_words, xo_scales, w2_words, w2_scales, sa,
+    wb_words, wb_scales, wo_words, wo_scales, se, sf, offs, offs2, offs3, offs4, offs5, offs6, offs7, out,
+):
+    nc = tc.nc
+    with ExitStack() as ctx:
+        keep = ctx.enter_context(tc.tile_pool(name="keep", bufs=1))
+        psum = ctx.enter_context(tc.psum_pool(name="psum", bufs=1))
+
+        def sbuf(name, shape, dtype):
+            return keep.tile(shape, dtype, name=name, align_bytes=64)
+
+        def load_list(name, src):
+            tile = keep.tile(list(src.shape), U16, name=name)
+            nc.sync.dma_start(tile[:], src)
+            return tile
+
+        def load_e4m3(name, src):
+            tile = sbuf(name, [P, src.shape[2]], U32)
+            nc.sync.dma_start(tile[:].bitcast(I32), src[0].rearrange("p c t -> p (c t)").bitcast(I32))
+            return tile
+
+        def load_e2m1(name, src):
+            tile = sbuf(name, [P, src.shape[2] // 2], U16)
+            nc.sync.dma_start(tile[:].bitcast(I32), src[0].bitcast(I32))
+            return tile
+
+        def cleared_plane(name, src):
+            tile = sbuf(name, [P, src.shape[2]], U8)
+            nc.vector.memset(tile[:].bitcast(I32), 0)
+            return tile
+
+        def load_scales(tile, src):
+            for q in range(4):
+                nc.sync.dma_start(tile[32 * q : 32 * q + 4, :].bitcast(I32), src[0, 4 * q : 4 * q + 4, :].bitcast(I32))
+
+        def entries(tile, first, count):
+            return tile[:, first // PER_COLUMN : (first + count) // PER_COLUMN]
+
+        xt_s = cleared_plane("xt_s", xt_scales)
+        w_s = cleared_plane("w_s", w_scales)
+        xo_s = cleared_plane("xo_s", xo_scales)
+        w2_s = cleared_plane("w2_s", w2_scales)
+        wb_s = cleared_plane("wb_s", wb_scales)
+        wo_s = cleared_plane("wo_s", wo_scales)
+        pages = [[sbuf(f"page{k}_{nt}", [P, U], F32) for k in range(2)] for nt in range(N // P)]
+        for nt in range(N // P):
+            for k in range(2):
+                nc.vector.memset(pages[nt][k][:], 0.0)
+
+        l1 = load_list("l1", offs)
+        xt_w = load_e2m1("xt_w", xt_words)
+        load_scales(xt_s, xt_scales)
+        w_w = load_e4m3("w_w", w_words)
+        xo_w = load_e4m3("xo_w", xo_words)
+        load_scales(w_s, w_scales)
+        l2 = load_list("l2", offs2)
+        load_scales(xo_s, xo_scales)
+        w2_w = load_e2m1("w2_w", w2_words)
+        load_scales(w2_s, w2_scales)
+        l3 = load_list("l3", offs3)
+        sa_t = sbuf("sa_t", [P, PACK], F32)
+        nc.sync.dma_start(sa_t[:], sa.rearrange("(p t) o -> p (t o)", t=PACK))
+        wb_w = load_e2m1("wb_w", wb_words)
+        wo_w = load_e4m3("wo_w", wo_words)
+        load_scales(wb_s, wb_scales)
+        load_scales(wo_s, wo_scales)
+        l4 = load_list("l4", offs4)
+        l5 = load_list("l5", offs5)
+        l6 = load_list("l6", offs6)
+        l7 = load_list("l7", offs7)
+        se_t = sbuf("se_t", [P, N // P], F32)
+        sf_t = sbuf("sf_t", [P, N // P], F32)
+        with nc.allow_non_contiguous_dma(reason="one weight a partition and output tile"):
+            nc.sync.dma_start(se_t[:], se.rearrange("(t p) o -> p (t o)", p=P))
+            nc.sync.dma_start(sf_t[:], sf.rearrange("(t p) o -> p (t o)", p=P))
+
+        w_wd = sbuf("w_wd", [P, R], U32)
+        w_sd = sbuf("w_sd", [P, R], U8)
+        w2_wd = sbuf("w2_wd", [P, R], U16)
+        w2_sd = sbuf("w2_sd", [P, R], U8)
+        for src, dst in ((w_w, w_wd), (w2_w, w2_wd)):
+            nc.scalar.copy(dst[:].rearrange("p (t m) -> p m t", t=PACK), src[:].rearrange("p (m t) -> p m t", t=PACK))
+        for src, dst in ((w_s, w_sd), (w2_s, w2_sd)):
+            nc.gpsimd.tensor_copy(dst[:].rearrange("p (t m) -> p t m", t=PACK), src[:].rearrange("p (m t) -> p t m", t=PACK))
+
+        xt_wg = sbuf("xt_wg", [P, J], U16)
+        xt_sg = sbuf("xt_sg", [P, J], U8)
+        xo_wg = sbuf("xo_wg", [P, J], U32)
+        xo_sg = sbuf("xo_sg", [P, J], U8)
+        jh = J // HALVES
+        nc.vector.tensor_copy(xt_wg[:], xt_w[:].indirect(l1[:]))
+        nc.vector.tensor_copy(xt_sg[:], xt_s[:].indirect(l1[:]))
+        nc.vector.tensor_copy(xo_wg[:], xo_w[:].indirect(l2[:]))
+        for h in range(HALVES):
+            nc.vector.tensor_copy(xo_sg[:, h * jh : (h + 1) * jh], xo_s[:].indirect(entries(l2, h * jh, jh)))
+
+        acc = [[psum.tile([P, jh], F32, name=f"acc{h}_{t}", tag=f"bank{h}_{t}") for t in range(PACK)] for h in range(HALVES)]
+        g1 = [sbuf(f"g1_{t}", [P, J], F32) for t in range(PACK)]
+        for h in range(HALVES):
+            js = slice(h * jh, (h + 1) * jh)
+            for t in range(PACK):
+                rs = slice(t * P, (t + 1) * P)
+                nc.tensor.matmul_mx(
+                    acc[h][t][:], lhsT=w_wd[:, rs].bitcast(FP8X4), lhsT_scale=w_sd[:, rs],
+                    rhs=xt_wg[:, js].bitcast(FP4X4), rhs_scale=xt_sg[:, js], start=True, stop=False,
+                )
+        for h in range(HALVES):
+            js = slice(h * jh, (h + 1) * jh)
+            for t in range(PACK):
+                rs = slice(t * P, (t + 1) * P)
+                nc.tensor.matmul_mx(
+                    acc[h][t][:], lhsT=w2_wd[:, rs].bitcast(FP4X4), lhsT_scale=w2_sd[:, rs],
+                    rhs=xo_wg[:, js].bitcast(FP8X4), rhs_scale=xo_sg[:, js], start=False, stop=True,
+                )
+                if h == 0:
+                    nc.scalar.activation(g1[t][:, js], acc[h][t][:], ACT.Relu)
+                else:
+                    nc.vector.tensor_scalar_max(g1[t][:, js], acc[h][t][:], 0.0)
+
+        oh = O // HALVES
+        hid = [sbuf(f"hid{h}", [P, PACK, oh], BF16) for h in range(HALVES)]
+        for h in range(HALVES):
+            for t in range(PACK):
+                nc.scalar.activation(
+                    hid[h][:, t, :], g1[t][:].indirect(entries(l3, h * oh, oh)), ACT.Copy, scale=sa_t[:, t : t + 1]
+                )
+
+        res_ps = [[psum.tile([P, O], F32, name=f"res{k}_{nt}", tag=f"bank0_{2 * nt + k}") for k in range(2)] for nt in range(N // P)]
+        res = [[sbuf(f"res_sb{k}_{nt}", [P, O], F32) for k in range(2)] for nt in range(N // P)]
+        second = ((wb_w, wb_s, FP4X4), (wo_w, wo_s, FP8X4))
+        for h in range(HALVES):
+            os_ = slice(h * oh, (h + 1) * oh)
+            woven = sbuf(f"woven{h}", [P, oh, PACK], BF16)
+            nc.vector.tensor_copy(woven[:], hid[h][:].rearrange("p t c -> p c t"))
+            codes = sbuf(f"codes{h}", [P, oh], U32)
+            plane = sbuf(f"plane{h}", [P, oh], U8)
+            nc.vector.quantize_mx(out=codes[:].bitcast(FP8X4), scales=plane[:], in_=woven[:].rearrange("p c t -> p (c t)"))
+            for nt in range(N // P):
+                ns = slice(nt * P, (nt + 1) * P)
+                for k, (words, scales, fmt) in enumerate(second):
+                    nc.tensor.matmul_mx(
+                        res_ps[nt][k][:, os_], lhsT=words[:, ns].bitcast(fmt), lhsT_scale=scales[:, ns],
+                        rhs=codes[:].bitcast(FP8X4), rhs_scale=plane[:], start=True, stop=True,
+                    )
+                    nc.vector.tensor_copy(res[nt][k][:, os_], res_ps[nt][k][:, os_])
+
+        put = (l4, l5)
+        for h in range(HALVES):
+            for k in range(2):
+                nc.scalar.activation(
+                    pages[0][k][:].indirect(entries(put[k], h * oh, oh)), res[0][k][:, h * oh : (h + 1) * oh], ACT.Copy
+                )
+        for k in range(2):
+            nc.scalar.activation(pages[1][k][:].indirect(put[k][:]), res[1][k][:], ACT.Copy)
+
+        larger = [sbuf(f"larger{nt}", [P, U], F32) for nt in range(N // P)]
+        for nt in range(N // P):
+            nc.vector.tensor_tensor(larger[nt][:], pages[nt][0][:], pages[nt][1][:], ALU.max)
+        plus = [sbuf(f"plus{nt}", [P, E], F32) for nt in range(N // P)]
+        minus = [sbuf(f"minus{nt}", [P, E], F32) for nt in range(N // P)]
+        for nt in range(N // P):
+            nc.scalar.activation(minus[nt][:], pages[nt][1][:].indirect(l7[:]), ACT.Copy, scale=sf_t[:, nt : nt + 1])
+        for nt in range(N // P):
+            nc.scalar.activation(plus[nt][:], larger[nt][:].indirect(l6[:]), ACT.Copy, scale=se_t[:, nt : nt + 1])
+            y = sbuf(f"y{nt}", [P, E], F32)
+            nc.vector.tensor_tensor(y[:], plus[nt][:], minus[nt][:], ALU.subtract)
+            nc.sync.dma_start(out[nt * P : (nt + 1) * P, :], y[:])

@@ -48,9 +48,16 @@ def tile_picked_tokens_plain_bank_kept_outcomes_endreads_kernel(
             nc.sync.dma_start(tile[:].bitcast(I32), src[0].bitcast(I32))
             return tile
 
-        def cleared_plane(name, src):
+        def load_repeated(name, src):
             tile = sbuf(name, [P, src.shape[2]], U8)
-            nc.vector.memset(tile[:].bitcast(I32), 0)
+            for q in range(4):
+                rows = src[0, 4 * q : 4 * q + 4, :].bitcast(I32)
+                nc.sync.dma_start(tile[32 * q : 32 * q + 32, :].bitcast(I32), rows.unsqueeze(0).to_broadcast([8, 4, src.shape[2] // 4]))
+            return tile
+
+        def cleared_plane(name, src, engine=nc.gpsimd):
+            tile = sbuf(name, [P, src.shape[2]], U8)
+            engine.memset(tile[:].bitcast(I32), 0)
             return tile
 
         def load_scales(tile, src):
@@ -60,30 +67,39 @@ def tile_picked_tokens_plain_bank_kept_outcomes_endreads_kernel(
         def entries(tile, first, count):
             return tile[:, first // PER_COLUMN : (first + count) // PER_COLUMN]
 
-        xt_s = cleared_plane("xt_s", xt_scales)
-        w_s = cleared_plane("w_s", w_scales)
-        xo_s = cleared_plane("xo_s", xo_scales)
+        def load_staged(name, src):
+            tile = sbuf(name, [4, 4, src.shape[2] // 4], I32)
+            nc.sync.dma_start(tile[:], src[0].bitcast(I32).rearrange("(q r) c -> r q c", r=4))
+            return tile
+
+        def spread_staged(staged, plane):
+            for q in range(4):
+                nc.vector.tensor_copy(plane[32 * q : 32 * q + 4, :].bitcast(I32), staged[:, q, :])
+
         w2_s = cleared_plane("w2_s", w2_scales)
+        w_s = cleared_plane("w_s", w_scales)
+        xt_s = cleared_plane("xt_s", xt_scales, nc.vector)
         wb_s = cleared_plane("wb_s", wb_scales)
         wo_s = cleared_plane("wo_s", wo_scales)
         pages = [[sbuf(f"page{k}_{nt}", [P, U], F32) for k in range(2)] for nt in range(N // P)]
         for nt in range(N // P):
             for k in range(2):
-                nc.vector.memset(pages[nt][k][:], 0.0)
+                nc.gpsimd.memset(pages[nt][k][:], 0.0)
 
+        w2_rows = load_staged("w2_rows", w2_scales)
+        l2 = load_list("l2", offs2)
+        xo_s = load_repeated("xo_s", xo_scales)
+        xo_w = load_e4m3("xo_w", xo_words)
+        w2_w = load_e2m1("w2_w", w2_words)
+        w_rows = load_staged("w_rows", w_scales)
         l1 = load_list("l1", offs)
         xt_w = load_e2m1("xt_w", xt_words)
-        load_scales(xt_s, xt_scales)
         w_w = load_e4m3("w_w", w_words)
-        xo_w = load_e4m3("xo_w", xo_words)
-        load_scales(w_s, w_scales)
-        l2 = load_list("l2", offs2)
-        load_scales(xo_s, xo_scales)
-        w2_w = load_e2m1("w2_w", w2_words)
-        load_scales(w2_s, w2_scales)
+        load_scales(xt_s, xt_scales)
         l3 = load_list("l3", offs3)
-        sa_t = sbuf("sa_t", [P, PACK], F32)
-        nc.sync.dma_start(sa_t[:], sa.rearrange("(p t) o -> p (t o)", t=PACK))
+        sa_t = [keep.tile([P, PACK], F32, name=f"sa{h}", tag=f"sa{h}", align_bytes=64) for h in range(HALVES)]
+        for h in range(HALVES):
+            nc.sync.dma_start(sa_t[h][:], sa.rearrange("(p t) o -> p (t o)", t=PACK))
         wb_w = load_e2m1("wb_w", wb_words)
         wo_w = load_e4m3("wo_w", wo_words)
         load_scales(wb_s, wb_scales)
@@ -102,21 +118,23 @@ def tile_picked_tokens_plain_bank_kept_outcomes_endreads_kernel(
         w_sd = sbuf("w_sd", [P, R], U8)
         w2_wd = sbuf("w2_wd", [P, R], U16)
         w2_sd = sbuf("w2_sd", [P, R], U8)
-        for src, dst in ((w_w, w_wd), (w2_w, w2_wd)):
-            nc.scalar.copy(dst[:].rearrange("p (t m) -> p m t", t=PACK), src[:].rearrange("p (m t) -> p m t", t=PACK))
-        for src, dst in ((w_s, w_sd), (w2_s, w2_sd)):
-            nc.gpsimd.tensor_copy(dst[:].rearrange("p (t m) -> p t m", t=PACK), src[:].rearrange("p (m t) -> p t m", t=PACK))
-
         xt_wg = sbuf("xt_wg", [P, J], U16)
         xt_sg = sbuf("xt_sg", [P, J], U8)
         xo_wg = sbuf("xo_wg", [P, J], U32)
         xo_sg = sbuf("xo_sg", [P, J], U8)
         jh = J // HALVES
-        nc.vector.tensor_copy(xt_wg[:], xt_w[:].indirect(l1[:]))
-        nc.vector.tensor_copy(xt_sg[:], xt_s[:].indirect(l1[:]))
-        nc.vector.tensor_copy(xo_wg[:], xo_w[:].indirect(l2[:]))
+        spread_staged(w2_rows, w2_s)
+        nc.vector.tensor_copy(xo_sg[:], xo_s[:].indirect(l2[:]))
         for h in range(HALVES):
-            nc.vector.tensor_copy(xo_sg[:, h * jh : (h + 1) * jh], xo_s[:].indirect(entries(l2, h * jh, jh)))
+            nc.vector.tensor_copy(xo_wg[:, h * jh : (h + 1) * jh], xo_w[:].indirect(entries(l2, h * jh, jh)))
+        spread_staged(w_rows, w_s)
+        for h in range(HALVES):
+            nc.vector.tensor_copy(xt_wg[:, h * jh : (h + 1) * jh], xt_w[:].indirect(entries(l1, h * jh, jh)))
+            nc.vector.tensor_copy(xt_sg[:, h * jh : (h + 1) * jh], xt_s[:].indirect(entries(l1, h * jh, jh)))
+        for src, dst in ((w2_w, w2_wd), (w_w, w_wd)):
+            nc.scalar.copy(dst[:].rearrange("p (t m) -> p m t", t=PACK), src[:].rearrange("p (m t) -> p m t", t=PACK))
+        for src, dst in ((w2_s, w2_sd), (w_s, w_sd)):
+            nc.gpsimd.tensor_copy(dst[:].rearrange("p (t m) -> p t m", t=PACK), src[:].rearrange("p (m t) -> p t m", t=PACK))
 
         acc = [[psum.tile([P, jh], F32, name=f"acc{h}_{t}", tag=f"bank{h}_{t}") for t in range(PACK)] for h in range(HALVES)]
         g1 = [sbuf(f"g1_{t}", [P, J], F32) for t in range(PACK)]
@@ -125,16 +143,16 @@ def tile_picked_tokens_plain_bank_kept_outcomes_endreads_kernel(
             for t in range(PACK):
                 rs = slice(t * P, (t + 1) * P)
                 nc.tensor.matmul_mx(
-                    acc[h][t][:], lhsT=w_wd[:, rs].bitcast(FP8X4), lhsT_scale=w_sd[:, rs],
-                    rhs=xt_wg[:, js].bitcast(FP4X4), rhs_scale=xt_sg[:, js], start=True, stop=False,
+                    acc[h][t][:], lhsT=w2_wd[:, rs].bitcast(FP4X4), lhsT_scale=w2_sd[:, rs],
+                    rhs=xo_wg[:, js].bitcast(FP8X4), rhs_scale=xo_sg[:, js], start=True, stop=False,
                 )
         for h in range(HALVES):
             js = slice(h * jh, (h + 1) * jh)
             for t in range(PACK):
                 rs = slice(t * P, (t + 1) * P)
                 nc.tensor.matmul_mx(
-                    acc[h][t][:], lhsT=w2_wd[:, rs].bitcast(FP4X4), lhsT_scale=w2_sd[:, rs],
-                    rhs=xo_wg[:, js].bitcast(FP8X4), rhs_scale=xo_sg[:, js], start=False, stop=True,
+                    acc[h][t][:], lhsT=w_wd[:, rs].bitcast(FP8X4), lhsT_scale=w_sd[:, rs],
+                    rhs=xt_wg[:, js].bitcast(FP4X4), rhs_scale=xt_sg[:, js], start=False, stop=True,
                 )
                 if h == 0:
                     nc.scalar.activation(g1[t][:, js], acc[h][t][:], ACT.Relu)
@@ -142,11 +160,12 @@ def tile_picked_tokens_plain_bank_kept_outcomes_endreads_kernel(
                     nc.vector.tensor_scalar_max(g1[t][:, js], acc[h][t][:], 0.0)
 
         oh = O // HALVES
-        hid = [sbuf(f"hid{h}", [P, PACK, oh], BF16) for h in range(HALVES)]
+        hid = []
         for h in range(HALVES):
+            hid.append(keep.tile([P, PACK, oh], BF16, name=f"hid{h}", tag="hid0" if h == 0 else "sa0", align_bytes=64))
             for t in range(PACK):
                 nc.scalar.activation(
-                    hid[h][:, t, :], g1[t][:].indirect(entries(l3, h * oh, oh)), ACT.Copy, scale=sa_t[:, t : t + 1]
+                    hid[h][:, t, :], g1[t][:].indirect(entries(l3, h * oh, oh)), ACT.Copy, scale=sa_t[h][:, t : t + 1]
                 )
 
         res_ps = [[psum.tile([P, O], F32, name=f"res{k}_{nt}", tag=f"bank0_{2 * nt + k}") for k in range(2)] for nt in range(N // P)]
@@ -154,9 +173,9 @@ def tile_picked_tokens_plain_bank_kept_outcomes_endreads_kernel(
         second = ((wb_w, wb_s, FP4X4), (wo_w, wo_s, FP8X4))
         for h in range(HALVES):
             os_ = slice(h * oh, (h + 1) * oh)
-            woven = sbuf(f"woven{h}", [P, oh, PACK], BF16)
+            woven = keep.tile([P, oh, PACK], BF16, name=f"woven{h}", tag="woven0" if h == 0 else "codes0", align_bytes=64)
             nc.vector.tensor_copy(woven[:], hid[h][:].rearrange("p t c -> p c t"))
-            codes = sbuf(f"codes{h}", [P, oh], U32)
+            codes = keep.tile([P, oh], U32, name=f"codes{h}", tag=f"codes{h}", align_bytes=64)
             plane = sbuf(f"plane{h}", [P, oh], U8)
             nc.vector.quantize_mx(out=codes[:].bitcast(FP8X4), scales=plane[:], in_=woven[:].rearrange("p c t -> p (c t)"))
             for nt in range(N // P):
@@ -184,7 +203,6 @@ def tile_picked_tokens_plain_bank_kept_outcomes_endreads_kernel(
         minus = [sbuf(f"minus{nt}", [P, E], F32) for nt in range(N // P)]
         for nt in range(N // P):
             nc.scalar.activation(minus[nt][:], pages[nt][1][:].indirect(l7[:]), ACT.Copy, scale=sf_t[:, nt : nt + 1])
-        for nt in range(N // P):
             nc.scalar.activation(plus[nt][:], larger[nt][:].indirect(l6[:]), ACT.Copy, scale=se_t[:, nt : nt + 1])
             y = sbuf(f"y{nt}", [P, E], F32)
             nc.vector.tensor_tensor(y[:], plus[nt][:], minus[nt][:], ALU.subtract)

@@ -48,14 +48,7 @@ def tile_picked_tokens_plain_bank_kept_outcomes_endreads_kernel(
             nc.sync.dma_start(tile[:].bitcast(I32), src[0].bitcast(I32))
             return tile
 
-        def load_repeated(name, src):
-            tile = sbuf(name, [P, src.shape[2]], U8)
-            for q in range(4):
-                rows = src[0, 4 * q : 4 * q + 4, :].bitcast(I32)
-                nc.sync.dma_start(tile[32 * q : 32 * q + 32, :].bitcast(I32), rows.unsqueeze(0).to_broadcast([8, 4, src.shape[2] // 4]))
-            return tile
-
-        def cleared_plane(name, src, engine=nc.gpsimd):
+        def cleared_plane(name, src, engine):
             tile = sbuf(name, [P, src.shape[2]], U8)
             engine.memset(tile[:].bitcast(I32), 0)
             return tile
@@ -67,31 +60,37 @@ def tile_picked_tokens_plain_bank_kept_outcomes_endreads_kernel(
         def entries(tile, first, count):
             return tile[:, first // PER_COLUMN : (first + count) // PER_COLUMN]
 
-        def load_staged(name, src):
-            tile = sbuf(name, [4, 4, src.shape[2] // 4], I32)
-            nc.sync.dma_start(tile[:], src[0].bitcast(I32).rearrange("(q r) c -> r q c", r=4))
+        def staged_plane(name, src, engine):
+            tile = sbuf(name, [P, 2, src.shape[2]], U8)
+            engine.memset(tile[:].rearrange("p a c -> p (a c)").bitcast(I32), 0)
             return tile
 
-        def spread_staged(staged, plane):
-            for q in range(4):
-                nc.vector.tensor_copy(plane[32 * q : 32 * q + 4, :].bitcast(I32), staged[:, q, :])
+        def load_staged(tile, src):
+            rows = src[0].bitcast(I32).rearrange("(a b r) c -> b r a c", b=2, r=4)
+            for b in range(2):
+                nc.sync.dma_start(tile[32 * b : 32 * b + 4, :, :].bitcast(I32), rows[b])
 
-        w2_s = cleared_plane("w2_s", w2_scales)
-        w_s = cleared_plane("w_s", w_scales)
+        def spread_staged(tile):
+            words = tile[:].bitcast(I32)
+            nc.vector.tensor_copy(words[64:128, 0, :], words[0:64, 1, :])
+
+        xo_s = cleared_plane("xo_s", xo_scales, nc.gpsimd)
+        w2_s = staged_plane("w2_s", w2_scales, nc.gpsimd)
+        w_s = staged_plane("w_s", w_scales, nc.gpsimd)
         xt_s = cleared_plane("xt_s", xt_scales, nc.vector)
-        wb_s = cleared_plane("wb_s", wb_scales)
-        wo_s = cleared_plane("wo_s", wo_scales)
+        wb_s = cleared_plane("wb_s", wb_scales, nc.vector)
+        wo_s = cleared_plane("wo_s", wo_scales, nc.vector)
         pages = [[sbuf(f"page{k}_{nt}", [P, U], F32) for k in range(2)] for nt in range(N // P)]
         for nt in range(N // P):
             for k in range(2):
-                nc.gpsimd.memset(pages[nt][k][:], 0.0)
+                nc.vector.memset(pages[nt][k][:], 0.0)
 
-        w2_rows = load_staged("w2_rows", w2_scales)
         l2 = load_list("l2", offs2)
-        xo_s = load_repeated("xo_s", xo_scales)
+        load_scales(xo_s, xo_scales)
+        load_staged(w2_s, w2_scales)
         xo_w = load_e4m3("xo_w", xo_words)
         w2_w = load_e2m1("w2_w", w2_words)
-        w_rows = load_staged("w_rows", w_scales)
+        load_staged(w_s, w_scales)
         l1 = load_list("l1", offs)
         xt_w = load_e2m1("xt_w", xt_words)
         w_w = load_e4m3("w_w", w_words)
@@ -123,18 +122,28 @@ def tile_picked_tokens_plain_bank_kept_outcomes_endreads_kernel(
         xo_wg = sbuf("xo_wg", [P, J], U32)
         xo_sg = sbuf("xo_sg", [P, J], U8)
         jh = J // HALVES
-        spread_staged(w2_rows, w2_s)
+
+        def deal(copy, dst, src):
+            copy(dst.rearrange("p (t m) -> p m t", t=PACK), src.rearrange("p (m t) -> p m t", t=PACK))
+
+        def gather(dst, window, offsets, h):
+            nc.vector.tensor_copy(dst[:, h * jh : (h + 1) * jh], window[:].indirect(entries(offsets, h * jh, jh)))
+
+        def deal_bytes(dst, src):
+            nc.gpsimd.tensor_copy(dst.rearrange("p (t m) -> p t m", t=PACK), src.rearrange("p (m t) -> p t m", t=PACK))
+
         nc.vector.tensor_copy(xo_sg[:], xo_s[:].indirect(l2[:]))
+        spread_staged(w2_s)
+        deal_bytes(w2_sd[:], w2_s[:, 0, :])
+        gather(xo_wg, xo_w, l2, 0)
+        spread_staged(w_s)
+        deal_bytes(w_sd[:], w_s[:, 0, :])
+        gather(xo_wg, xo_w, l2, 1)
+        nc.vector.tensor_copy(xt_wg[:], xt_w[:].indirect(l1[:]))
         for h in range(HALVES):
-            nc.vector.tensor_copy(xo_wg[:, h * jh : (h + 1) * jh], xo_w[:].indirect(entries(l2, h * jh, jh)))
-        spread_staged(w_rows, w_s)
-        for h in range(HALVES):
-            nc.vector.tensor_copy(xt_wg[:, h * jh : (h + 1) * jh], xt_w[:].indirect(entries(l1, h * jh, jh)))
-            nc.vector.tensor_copy(xt_sg[:, h * jh : (h + 1) * jh], xt_s[:].indirect(entries(l1, h * jh, jh)))
-        for src, dst in ((w2_w, w2_wd), (w_w, w_wd)):
-            nc.scalar.copy(dst[:].rearrange("p (t m) -> p m t", t=PACK), src[:].rearrange("p (m t) -> p m t", t=PACK))
-        for src, dst in ((w2_s, w2_sd), (w_s, w_sd)):
-            nc.gpsimd.tensor_copy(dst[:].rearrange("p (t m) -> p t m", t=PACK), src[:].rearrange("p (m t) -> p t m", t=PACK))
+            gather(xt_sg, xt_s, l1, h)
+        deal(nc.scalar.copy, w2_wd[:], w2_w[:])
+        deal(nc.scalar.copy, w_wd[:], w_w[:])
 
         acc = [[psum.tile([P, jh], F32, name=f"acc{h}_{t}", tag=f"bank{h}_{t}") for t in range(PACK)] for h in range(HALVES)]
         g1 = [sbuf(f"g1_{t}", [P, J], F32) for t in range(PACK)]
@@ -154,7 +163,7 @@ def tile_picked_tokens_plain_bank_kept_outcomes_endreads_kernel(
                     acc[h][t][:], lhsT=w_wd[:, rs].bitcast(FP8X4), lhsT_scale=w_sd[:, rs],
                     rhs=xt_wg[:, js].bitcast(FP4X4), rhs_scale=xt_sg[:, js], start=False, stop=True,
                 )
-                if h == 0:
+                if h == 0 and t < PACK - 1:
                     nc.scalar.activation(g1[t][:, js], acc[h][t][:], ACT.Relu)
                 else:
                     nc.vector.tensor_scalar_max(g1[t][:, js], acc[h][t][:], 0.0)
@@ -188,13 +197,13 @@ def tile_picked_tokens_plain_bank_kept_outcomes_endreads_kernel(
                     nc.vector.tensor_copy(res[nt][k][:, os_], res_ps[nt][k][:, os_])
 
         put = (l4, l5)
+        halved = ((0, 0), (0, 1), (1, 0))
         for h in range(HALVES):
-            for k in range(2):
+            for nt, k in halved:
                 nc.scalar.activation(
-                    pages[0][k][:].indirect(entries(put[k], h * oh, oh)), res[0][k][:, h * oh : (h + 1) * oh], ACT.Copy
+                    pages[nt][k][:].indirect(entries(put[k], h * oh, oh)), res[nt][k][:, h * oh : (h + 1) * oh], ACT.Copy
                 )
-        for k in range(2):
-            nc.scalar.activation(pages[1][k][:].indirect(put[k][:]), res[1][k][:], ACT.Copy)
+        nc.scalar.activation(pages[1][1][:].indirect(l5[:]), res[1][1][:], ACT.Copy)
 
         larger = [sbuf(f"larger{nt}", [P, U], F32) for nt in range(N // P)]
         for nt in range(N // P):

@@ -13,11 +13,18 @@ FP4X4 = mybir.dt.float4_e2m1fn_x4
 ACT = mybir.ActivationFunctionType
 ALU = mybir.AluOpType
 
-K, J, R, T, Z, M, O, N, U, E = 512, 512, 512, 2048, 512, 1024, 256, 256, 512, 128
+K, J, R, Z, O, N, U, E = 512, 512, 512, 512, 256, 256, 512, 128
 P = 128
 PACK = 4
+QUADRANTS = 4
+QUADRANT = P // QUADRANTS
+LIVE_ROWS = 4
 PER_COLUMN = 16
+LINE_BYTES = 16
 HALVES = 2
+J_HALF = J // HALVES
+O_HALF = O // HALVES
+OUT_TILES = N // P
 FLOPS = 2 * (K * R * J + Z * R * J + 2 * R * N * O)
 
 
@@ -30,8 +37,8 @@ def tile_picked_tokens_plain_bank_kept_outcomes_endreads_kernel(
         keep = ctx.enter_context(tc.tile_pool(name="keep", bufs=1))
         psum = ctx.enter_context(tc.psum_pool(name="psum", bufs=1))
 
-        def sbuf(name, shape, dtype):
-            return keep.tile(shape, dtype, name=name, align_bytes=64)
+        def sbuf(name, shape, dtype, tag=None):
+            return keep.tile(shape, dtype, name=name, tag=tag or name, align_bytes=64)
 
         def load_list(name, src):
             tile = keep.tile(list(src.shape), U16, name=name)
@@ -53,166 +60,195 @@ def tile_picked_tokens_plain_bank_kept_outcomes_endreads_kernel(
             engine.memset(tile[:].bitcast(I32), 0)
             return tile
 
-        def load_scales(tile, src):
-            for q in range(4):
-                nc.sync.dma_start(tile[32 * q : 32 * q + 4, :].bitcast(I32), src[0, 4 * q : 4 * q + 4, :].bitcast(I32))
+        def load_plane(tile, src):
+            for q in range(QUADRANTS):
+                rows = src[0, LIVE_ROWS * q : LIVE_ROWS * (q + 1), :]
+                nc.sync.dma_start(tile[QUADRANT * q : QUADRANT * q + LIVE_ROWS, :].bitcast(I32), rows.bitcast(I32))
 
-        def entries(tile, first, count):
-            return tile[:, first // PER_COLUMN : (first + count) // PER_COLUMN]
-
-        def staged_plane(name, src, engine):
+        def cleared_folded_plane(name, src):
             tile = sbuf(name, [P, 2, src.shape[2]], U8)
-            engine.memset(tile[:].rearrange("p a c -> p (a c)").bitcast(I32), 0)
+            nc.gpsimd.memset(tile[:].rearrange("p f c -> p (f c)").bitcast(I32), 0)
             return tile
 
-        def load_staged(tile, src):
-            rows = src[0].bitcast(I32).rearrange("(a b r) c -> b r a c", b=2, r=4)
+        def load_folded_plane(tile, src):
+            rows = src[0].bitcast(I32).rearrange("(f b i) c -> b i f c", b=2, i=LIVE_ROWS)
             for b in range(2):
-                nc.sync.dma_start(tile[32 * b : 32 * b + 4, :, :].bitcast(I32), rows[b])
+                nc.sync.dma_start(tile[QUADRANT * b : QUADRANT * b + LIVE_ROWS, :, :].bitcast(I32), rows[b])
 
-        def spread_staged(tile):
-            words = tile[:].bitcast(I32)
-            nc.vector.tensor_copy(words[64:128, 0, :], words[0:64, 1, :])
+        def unfold_plane(tile):
+            as_words = tile[:].bitcast(I32)
+            nc.vector.tensor_copy(as_words[P // 2 : P, 0, :], as_words[0 : P // 2, 1, :])
 
-        xo_s = cleared_plane("xo_s", xo_scales, nc.gpsimd)
-        w2_s = staged_plane("w2_s", w2_scales, nc.gpsimd)
-        w_s = staged_plane("w_s", w_scales, nc.gpsimd)
-        xt_s = cleared_plane("xt_s", xt_scales, nc.vector)
-        wb_s = cleared_plane("wb_s", wb_scales, nc.vector)
-        wo_s = cleared_plane("wo_s", wo_scales, nc.vector)
-        pages = [[sbuf(f"page{k}_{nt}", [P, U], F32) for k in range(2)] for nt in range(N // P)]
-        for nt in range(N // P):
+        def entries(offsets, first, count):
+            return offsets[:, first // PER_COLUMN : (first + count) // PER_COLUMN]
+
+        xo_plane = cleared_plane("xo_plane", xo_scales, nc.gpsimd)
+        w2_folded = cleared_folded_plane("w2_folded", w2_scales)
+        w_folded = cleared_folded_plane("w_folded", w_scales)
+        xt_plane = cleared_plane("xt_plane", xt_scales, nc.vector)
+        wb_plane = cleared_plane("wb_plane", wb_scales, nc.vector)
+        wo_plane = cleared_plane("wo_plane", wo_scales, nc.vector)
+        pages = [[sbuf(f"page{k}_{nt}", [P, U], F32) for k in range(2)] for nt in range(OUT_TILES)]
+        for nt in range(OUT_TILES):
             for k in range(2):
                 nc.vector.memset(pages[nt][k][:], 0.0)
 
-        l2 = load_list("l2", offs2)
-        load_scales(xo_s, xo_scales)
-        load_staged(w2_s, w2_scales)
-        xo_w = load_e4m3("xo_w", xo_words)
-        w2_w = load_e2m1("w2_w", w2_words)
-        load_staged(w_s, w_scales)
-        l1 = load_list("l1", offs)
-        xt_w = load_e2m1("xt_w", xt_words)
-        w_w = load_e4m3("w_w", w_words)
-        load_scales(xt_s, xt_scales)
-        l3 = load_list("l3", offs3)
-        sa_t = [keep.tile([P, PACK], F32, name=f"sa{h}", tag=f"sa{h}", align_bytes=64) for h in range(HALVES)]
+        note_list = load_list("note_list", offs2)
+        load_plane(xo_plane, xo_scales)
+        load_folded_plane(w2_folded, w2_scales)
+        xo_codes = load_e4m3("xo_codes", xo_words)
+        w2_codes = load_e2m1("w2_codes", w2_words)
+        load_folded_plane(w_folded, w_scales)
+        token_list = load_list("token_list", offs)
+        xt_codes = load_e2m1("xt_codes", xt_words)
+        w_codes = load_e4m3("w_codes", w_words)
+        load_plane(xt_plane, xt_scales)
+        slot_list = load_list("slot_list", offs3)
+        sa_tiles = [sbuf(f"sa{h}", [P, PACK], F32) for h in range(HALVES)]
         for h in range(HALVES):
-            nc.sync.dma_start(sa_t[h][:], sa.rearrange("(p t) o -> p (t o)", t=PACK))
-        wb_w = load_e2m1("wb_w", wb_words)
-        wo_w = load_e4m3("wo_w", wo_words)
-        load_scales(wb_s, wb_scales)
-        load_scales(wo_s, wo_scales)
-        l4 = load_list("l4", offs4)
-        l5 = load_list("l5", offs5)
-        l6 = load_list("l6", offs6)
-        l7 = load_list("l7", offs7)
-        se_t = sbuf("se_t", [P, N // P], F32)
-        sf_t = sbuf("sf_t", [P, N // P], F32)
-        with nc.allow_non_contiguous_dma(reason="one weight a partition and output tile"):
-            nc.sync.dma_start(se_t[:], se.rearrange("(t p) o -> p (t o)", p=P))
-            nc.sync.dma_start(sf_t[:], sf.rearrange("(t p) o -> p (t o)", p=P))
+            nc.sync.dma_start(sa_tiles[h][:], sa.rearrange("(p t) o -> p (t o)", t=PACK))
+        wb_codes = load_e2m1("wb_codes", wb_words)
+        wo_codes = load_e4m3("wo_codes", wo_words)
+        load_plane(wb_plane, wb_scales)
+        load_plane(wo_plane, wo_scales)
+        put_lists = (load_list("put_p", offs4), load_list("put_q", offs5))
+        read_larger = load_list("read_larger", offs6)
+        read_second = load_list("read_second", offs7)
+        se_tile = sbuf("se_tile", [P, OUT_TILES], F32)
+        sf_tile = sbuf("sf_tile", [P, OUT_TILES], F32)
+        with nc.allow_non_contiguous_dma(reason="one weight for each partition and output tile"):
+            nc.sync.dma_start(se_tile[:], se.rearrange("(t p) o -> p (t o)", p=P))
+            nc.sync.dma_start(sf_tile[:], sf.rearrange("(t p) o -> p (t o)", p=P))
 
-        w_wd = sbuf("w_wd", [P, R], U32)
-        w_sd = sbuf("w_sd", [P, R], U8)
-        w2_wd = sbuf("w2_wd", [P, R], U16)
-        w2_sd = sbuf("w2_sd", [P, R], U8)
-        xt_wg = sbuf("xt_wg", [P, J], U16)
-        xt_sg = sbuf("xt_sg", [P, J], U8)
-        xo_wg = sbuf("xo_wg", [P, J], U32)
-        xo_sg = sbuf("xo_sg", [P, J], U8)
-        jh = J // HALVES
+        w_dealt = sbuf("w_dealt", [P, R], U32)
+        w_plane_dealt = sbuf("w_plane_dealt", [P, R], U8)
+        w2_dealt = sbuf("w2_dealt", [P, R], U16)
+        w2_plane_dealt = sbuf("w2_plane_dealt", [P, R], U8)
+        xt_picked = sbuf("xt_picked", [P, J], U16)
+        xt_plane_picked = sbuf("xt_plane_picked", [P, J], U8)
+        xo_picked = sbuf("xo_picked", [P, J], U32)
+        xo_plane_picked = sbuf("xo_plane_picked", [P, J], U8)
 
-        def deal(copy, dst, src):
-            copy(dst.rearrange("p (t m) -> p m t", t=PACK), src.rearrange("p (m t) -> p m t", t=PACK))
+        def deal_words(dst, src, word_bytes):
+            run = LINE_BYTES // word_bytes
+            nc.scalar.copy(
+                dst[:].rearrange("p (t b i) -> p b t i", t=PACK, i=run),
+                src[:].rearrange("p (b i t) -> p b t i", t=PACK, i=run),
+            )
 
-        def gather(dst, window, offsets, h):
-            nc.vector.tensor_copy(dst[:, h * jh : (h + 1) * jh], window[:].indirect(entries(offsets, h * jh, jh)))
+        def deal_plane(dst, folded):
+            nc.gpsimd.tensor_copy(
+                dst[:].rearrange("p (t m) -> p t m", t=PACK), folded[:, 0, :].rearrange("p (m t) -> p t m", t=PACK)
+            )
 
-        def deal_bytes(dst, src):
-            nc.gpsimd.tensor_copy(dst.rearrange("p (t m) -> p t m", t=PACK), src.rearrange("p (m t) -> p t m", t=PACK))
+        def gather_half(dst, window, offsets, h):
+            js = slice(h * J_HALF, (h + 1) * J_HALF)
+            nc.vector.tensor_copy(dst[:, js], window[:].indirect(entries(offsets, h * J_HALF, J_HALF)))
 
-        nc.vector.tensor_copy(xo_sg[:], xo_s[:].indirect(l2[:]))
-        spread_staged(w2_s)
-        deal_bytes(w2_sd[:], w2_s[:, 0, :])
-        gather(xo_wg, xo_w, l2, 0)
-        spread_staged(w_s)
-        deal_bytes(w_sd[:], w_s[:, 0, :])
-        gather(xo_wg, xo_w, l2, 1)
-        nc.vector.tensor_copy(xt_wg[:], xt_w[:].indirect(l1[:]))
+        nc.vector.tensor_copy(xo_plane_picked[:], xo_plane[:].indirect(note_list[:]))
+        unfold_plane(w2_folded)
+        deal_plane(w2_plane_dealt, w2_folded)
+        gather_half(xo_picked, xo_codes, note_list, 0)
+        unfold_plane(w_folded)
+        deal_plane(w_plane_dealt, w_folded)
+        gather_half(xo_picked, xo_codes, note_list, 1)
+        nc.vector.tensor_copy(xt_picked[:], xt_codes[:].indirect(token_list[:]))
         for h in range(HALVES):
-            gather(xt_sg, xt_s, l1, h)
-        deal(nc.scalar.copy, w2_wd[:], w2_w[:])
-        deal(nc.scalar.copy, w_wd[:], w_w[:])
+            gather_half(xt_plane_picked, xt_plane, token_list, h)
+        deal_words(w2_dealt, w2_codes, 2)
+        deal_words(w_dealt, w_codes, 4)
 
-        acc = [[psum.tile([P, jh], F32, name=f"acc{h}_{t}", tag=f"bank{h}_{t}") for t in range(PACK)] for h in range(HALVES)]
+        acc = [
+            [psum.tile([P, J_HALF], F32, name=f"acc{h}_{t}", tag=f"bank{h}_{t}") for t in range(PACK)]
+            for h in range(HALVES)
+        ]
         g1 = [sbuf(f"g1_{t}", [P, J], F32) for t in range(PACK)]
         for h in range(HALVES):
-            js = slice(h * jh, (h + 1) * jh)
+            js = slice(h * J_HALF, (h + 1) * J_HALF)
             for t in range(PACK):
                 rs = slice(t * P, (t + 1) * P)
                 nc.tensor.matmul_mx(
-                    acc[h][t][:], lhsT=w2_wd[:, rs].bitcast(FP4X4), lhsT_scale=w2_sd[:, rs],
-                    rhs=xo_wg[:, js].bitcast(FP8X4), rhs_scale=xo_sg[:, js], start=True, stop=False,
+                    acc[h][t][:], lhsT=w2_dealt[:, rs].bitcast(FP4X4), lhsT_scale=w2_plane_dealt[:, rs],
+                    rhs=xo_picked[:, js].bitcast(FP8X4), rhs_scale=xo_plane_picked[:, js], start=True, stop=False,
                 )
         for h in range(HALVES):
-            js = slice(h * jh, (h + 1) * jh)
+            js = slice(h * J_HALF, (h + 1) * J_HALF)
             for t in range(PACK):
                 rs = slice(t * P, (t + 1) * P)
                 nc.tensor.matmul_mx(
-                    acc[h][t][:], lhsT=w_wd[:, rs].bitcast(FP8X4), lhsT_scale=w_sd[:, rs],
-                    rhs=xt_wg[:, js].bitcast(FP4X4), rhs_scale=xt_sg[:, js], start=False, stop=True,
+                    acc[h][t][:], lhsT=w_dealt[:, rs].bitcast(FP8X4), lhsT_scale=w_plane_dealt[:, rs],
+                    rhs=xt_picked[:, js].bitcast(FP4X4), rhs_scale=xt_plane_picked[:, js], start=False, stop=True,
                 )
                 if h == 0 and t < PACK - 1:
                     nc.scalar.activation(g1[t][:, js], acc[h][t][:], ACT.Relu)
                 else:
                     nc.vector.tensor_scalar_max(g1[t][:, js], acc[h][t][:], 0.0)
 
-        oh = O // HALVES
         hid = []
         for h in range(HALVES):
-            hid.append(keep.tile([P, PACK, oh], BF16, name=f"hid{h}", tag="hid0" if h == 0 else "sa0", align_bytes=64))
+            hid.append(sbuf(f"hid{h}", [P, PACK, O_HALF], BF16, tag="hid0" if h == 0 else "sa0"))
             for t in range(PACK):
                 nc.scalar.activation(
-                    hid[h][:, t, :], g1[t][:].indirect(entries(l3, h * oh, oh)), ACT.Copy, scale=sa_t[h][:, t : t + 1]
+                    hid[h][:, t, :], g1[t][:].indirect(entries(slot_list, h * O_HALF, O_HALF)), ACT.Copy,
+                    scale=sa_tiles[h][:, t : t + 1],
                 )
 
-        res_ps = [[psum.tile([P, O], F32, name=f"res{k}_{nt}", tag=f"bank0_{2 * nt + k}") for k in range(2)] for nt in range(N // P)]
-        res = [[sbuf(f"res_sb{k}_{nt}", [P, O], F32) for k in range(2)] for nt in range(N // P)]
-        second = ((wb_w, wb_s, FP4X4), (wo_w, wo_s, FP8X4))
+        outcome_psum = [
+            [psum.tile([P, O], F32, name=f"outcome_psum{k}_{nt}", tag=f"bank0_{2 * nt + k}") for k in range(2)]
+            for nt in range(OUT_TILES)
+        ]
+        outcome = [[sbuf(f"outcome{k}_{nt}", [P, O], F32) for k in range(2)] for nt in range(OUT_TILES)]
+        matrices = ((wb_codes, wb_plane, FP4X4), (wo_codes, wo_plane, FP8X4))
         for h in range(HALVES):
-            os_ = slice(h * oh, (h + 1) * oh)
-            woven = keep.tile([P, oh, PACK], BF16, name=f"woven{h}", tag="woven0" if h == 0 else "codes0", align_bytes=64)
-            nc.vector.tensor_copy(woven[:], hid[h][:].rearrange("p t c -> p c t"))
-            codes = keep.tile([P, oh], U32, name=f"codes{h}", tag=f"codes{h}", align_bytes=64)
-            plane = sbuf(f"plane{h}", [P, oh], U8)
-            nc.vector.quantize_mx(out=codes[:].bitcast(FP8X4), scales=plane[:], in_=woven[:].rearrange("p c t -> p (c t)"))
-            for nt in range(N // P):
+            places = slice(h * O_HALF, (h + 1) * O_HALF)
+            woven = sbuf(f"woven{h}", [P, O_HALF, PACK], BF16, tag="woven0" if h == 0 else "hid_codes0")
+            hid_codes = sbuf(f"hid_codes{h}", [P, O_HALF], U32)
+            hid_plane = sbuf(f"hid_plane{h}", [P, O_HALF], U8)
+            pieces = [slice(c, c + O_HALF // 2) for c in (0, O_HALF // 2)]
+            for cs in pieces:
+                nc.vector.tensor_copy(
+                    woven[:, cs, :].rearrange("p (b i) t -> p b t i", i=PACK),
+                    hid[h][:, :, cs].rearrange("p t (b i) -> p b t i", i=PACK),
+                )
+            for cs in pieces:
+                nc.vector.quantize_mx(
+                    out=hid_codes[:, cs].bitcast(FP8X4), scales=hid_plane[:, cs],
+                    in_=woven[:, cs, :].rearrange("p c t -> p (c t)"),
+                )
+            for nt in range(OUT_TILES):
                 ns = slice(nt * P, (nt + 1) * P)
-                for k, (words, scales, fmt) in enumerate(second):
+                for k, (codes, plane, packed) in enumerate(matrices):
                     nc.tensor.matmul_mx(
-                        res_ps[nt][k][:, os_], lhsT=words[:, ns].bitcast(fmt), lhsT_scale=scales[:, ns],
-                        rhs=codes[:].bitcast(FP8X4), rhs_scale=plane[:], start=True, stop=True,
+                        outcome_psum[nt][k][:, places], lhsT=codes[:, ns].bitcast(packed), lhsT_scale=plane[:, ns],
+                        rhs=hid_codes[:].bitcast(FP8X4), rhs_scale=hid_plane[:], start=True, stop=True,
                     )
-                    nc.vector.tensor_copy(res[nt][k][:, os_], res_ps[nt][k][:, os_])
+                    nc.vector.tensor_copy(outcome[nt][k][:, places], outcome_psum[nt][k][:, places])
 
-        put = (l4, l5)
-        halved = ((0, 0), (0, 1), (1, 0))
+        page_order = [(nt, k) for nt in range(OUT_TILES) for k in range(2)]
+        last_nt, last_k = page_order[-1]
         for h in range(HALVES):
-            for nt, k in halved:
+            places = slice(h * O_HALF, (h + 1) * O_HALF)
+            for nt, k in page_order[:-1]:
                 nc.scalar.activation(
-                    pages[nt][k][:].indirect(entries(put[k], h * oh, oh)), res[nt][k][:, h * oh : (h + 1) * oh], ACT.Copy
+                    pages[nt][k][:].indirect(entries(put_lists[k], h * O_HALF, O_HALF)), outcome[nt][k][:, places],
+                    ACT.Copy,
                 )
-        nc.scalar.activation(pages[1][1][:].indirect(l5[:]), res[1][1][:], ACT.Copy)
+        nc.scalar.activation(
+            pages[last_nt][last_k][:].indirect(put_lists[last_k][:]), outcome[last_nt][last_k][:], ACT.Copy
+        )
 
-        larger = [sbuf(f"larger{nt}", [P, U], F32) for nt in range(N // P)]
-        for nt in range(N // P):
+        larger = [sbuf(f"larger{nt}", [P, U], F32) for nt in range(OUT_TILES)]
+        for nt in range(OUT_TILES):
             nc.vector.tensor_tensor(larger[nt][:], pages[nt][0][:], pages[nt][1][:], ALU.max)
-        plus = [sbuf(f"plus{nt}", [P, E], F32) for nt in range(N // P)]
-        minus = [sbuf(f"minus{nt}", [P, E], F32) for nt in range(N // P)]
-        for nt in range(N // P):
-            nc.scalar.activation(minus[nt][:], pages[nt][1][:].indirect(l7[:]), ACT.Copy, scale=sf_t[:, nt : nt + 1])
-            nc.scalar.activation(plus[nt][:], larger[nt][:].indirect(l6[:]), ACT.Copy, scale=se_t[:, nt : nt + 1])
+        plus = [sbuf(f"plus{nt}", [P, E], F32) for nt in range(OUT_TILES)]
+        minus = [sbuf(f"minus{nt}", [P, E], F32) for nt in range(OUT_TILES)]
+        for nt in range(OUT_TILES):
+            nc.scalar.activation(
+                minus[nt][:], pages[nt][1][:].indirect(read_second[:]), ACT.Copy, scale=sf_tile[:, nt : nt + 1]
+            )
+            nc.scalar.activation(
+                plus[nt][:], larger[nt][:].indirect(read_larger[:]), ACT.Copy, scale=se_tile[:, nt : nt + 1]
+            )
             y = sbuf(f"y{nt}", [P, E], F32)
             nc.vector.tensor_tensor(y[:], plus[nt][:], minus[nt][:], ALU.subtract)
             nc.sync.dma_start(out[nt * P : (nt + 1) * P, :], y[:])

from contextlib import ExitStack

import concourse.mybir as mybir

F32 = mybir.dt.float32
BF16 = mybir.dt.bfloat16
I32 = mybir.dt.int32
U32 = mybir.dt.uint32
U16 = mybir.dt.uint16
U8 = mybir.dt.uint8
FP8X4 = mybir.dt.float8_e4m3fn_x4
FP4X4 = mybir.dt.float4_e2m1fn_x4
ACT = mybir.ActivationFunctionType
ALU = mybir.AluOpType

K, J, R, Z, O, N, U, E = 512, 512, 512, 512, 256, 256, 512, 128
P = 128
PACK = 4
QUADRANTS = 4
QUADRANT = P // QUADRANTS
LIVE_ROWS = 4
PER_COLUMN = 16
LINE_BYTES = 16
HALVES = 2
J_HALF = J // HALVES
O_HALF = O // HALVES
OUT_TILES = N // P
FLOPS = 2 * (K * R * J + Z * R * J + 2 * R * N * O)


def tile_picked_tokens_plain_bank_kept_outcomes_endreads_kernel(
    tc, xt_words, xt_scales, w_words, w_scales, xo_words, xo_scales, w2_words, w2_scales, sa,
    wb_words, wb_scales, wo_words, wo_scales, se, sf, offs, offs2, offs3, offs4, offs5, offs6, offs7, out,
):
    nc = tc.nc
    with ExitStack() as ctx:
        keep = ctx.enter_context(tc.tile_pool(name="keep", bufs=1))
        psum = ctx.enter_context(tc.psum_pool(name="psum", bufs=1))

        def sbuf(name, shape, dtype, tag=None):
            return keep.tile(shape, dtype, name=name, tag=tag or name, align_bytes=64)

        def load_list(name, src):
            tile = keep.tile(list(src.shape), U16, name=name)
            nc.sync.dma_start(tile[:], src)
            return tile

        def load_e4m3(name, src):
            tile = sbuf(name, [P, src.shape[2]], U32)
            nc.sync.dma_start(tile[:].bitcast(I32), src[0].rearrange("p c t -> p (c t)").bitcast(I32))
            return tile

        def load_e2m1(name, src):
            tile = sbuf(name, [P, src.shape[2] // 2], U16)
            nc.sync.dma_start(tile[:].bitcast(I32), src[0].bitcast(I32))
            return tile

        def cleared_plane(name, src, engine):
            tile = sbuf(name, [P, src.shape[2]], U8)
            engine.memset(tile[:].bitcast(I32), 0)
            return tile

        def load_plane(tile, src):
            for q in range(QUADRANTS):
                rows = src[0, LIVE_ROWS * q : LIVE_ROWS * (q + 1), :]
                nc.sync.dma_start(tile[QUADRANT * q : QUADRANT * q + LIVE_ROWS, :].bitcast(I32), rows.bitcast(I32))

        def cleared_folded_plane(name, src):
            tile = sbuf(name, [P, 2, src.shape[2]], U8)
            nc.gpsimd.memset(tile[:].rearrange("p f c -> p (f c)").bitcast(I32), 0)
            return tile

        def load_folded_plane(tile, src):
            rows = src[0].bitcast(I32).rearrange("(f b i) c -> b i f c", b=2, i=LIVE_ROWS)
            for b in range(2):
                nc.sync.dma_start(tile[QUADRANT * b : QUADRANT * b + LIVE_ROWS, :, :].bitcast(I32), rows[b])

        def unfold_plane(tile):
            as_words = tile[:].bitcast(I32)
            nc.vector.tensor_copy(as_words[P // 2 : P, 0, :], as_words[0 : P // 2, 1, :])

        def entries(offsets, first, count):
            return offsets[:, first // PER_COLUMN : (first + count) // PER_COLUMN]

        xo_plane = cleared_plane("xo_plane", xo_scales, nc.gpsimd)
        w2_folded = cleared_folded_plane("w2_folded", w2_scales)
        w_folded = cleared_folded_plane("w_folded", w_scales)
        xt_plane = cleared_plane("xt_plane", xt_scales, nc.vector)
        wb_plane = cleared_plane("wb_plane", wb_scales, nc.vector)
        wo_plane = cleared_plane("wo_plane", wo_scales, nc.vector)
        pages = [[sbuf(f"page{k}_{nt}", [P, U], F32) for k in range(2)] for nt in range(OUT_TILES)]
        for nt in range(OUT_TILES):
            for k in range(2):
                nc.vector.memset(pages[nt][k][:], 0.0)

        note_list = load_list("note_list", offs2)
        load_plane(xo_plane, xo_scales)
        load_folded_plane(w2_folded, w2_scales)
        xo_codes = load_e4m3("xo_codes", xo_words)
        w2_codes = load_e2m1("w2_codes", w2_words)
        load_folded_plane(w_folded, w_scales)
        token_list = load_list("token_list", offs)
        xt_codes = load_e2m1("xt_codes", xt_words)
        w_codes = load_e4m3("w_codes", w_words)
        load_plane(xt_plane, xt_scales)
        slot_list = load_list("slot_list", offs3)
        sa_tiles = [sbuf(f"sa{h}", [P, PACK], F32) for h in range(HALVES)]
        for h in range(HALVES):
            nc.sync.dma_start(sa_tiles[h][:], sa.rearrange("(p t) o -> p (t o)", t=PACK))
        wb_codes = load_e2m1("wb_codes", wb_words)
        wo_codes = load_e4m3("wo_codes", wo_words)
        load_plane(wb_plane, wb_scales)
        load_plane(wo_plane, wo_scales)
        put_lists = (load_list("put_p", offs4), load_list("put_q", offs5))
        read_larger = load_list("read_larger", offs6)
        read_second = load_list("read_second", offs7)
        se_tile = sbuf("se_tile", [P, OUT_TILES], F32)
        sf_tile = sbuf("sf_tile", [P, OUT_TILES], F32)
        with nc.allow_non_contiguous_dma(reason="one weight for each partition and output tile"):
            nc.sync.dma_start(se_tile[:], se.rearrange("(t p) o -> p (t o)", p=P))
            nc.sync.dma_start(sf_tile[:], sf.rearrange("(t p) o -> p (t o)", p=P))

        w_dealt = sbuf("w_dealt", [P, R], U32)
        w_plane_dealt = sbuf("w_plane_dealt", [P, R], U8)
        w2_dealt = sbuf("w2_dealt", [P, R], U16)
        w2_plane_dealt = sbuf("w2_plane_dealt", [P, R], U8)
        xt_picked = sbuf("xt_picked", [P, J], U16)
        xt_plane_picked = sbuf("xt_plane_picked", [P, J], U8)
        xo_picked = sbuf("xo_picked", [P, J], U32)
        xo_plane_picked = sbuf("xo_plane_picked", [P, J], U8)

        def deal_words(dst, src, word_bytes):
            run = LINE_BYTES // word_bytes
            nc.scalar.copy(
                dst[:].rearrange("p (t b i) -> p b t i", t=PACK, i=run),
                src[:].rearrange("p (b i t) -> p b t i", t=PACK, i=run),
            )

        def deal_plane(dst, folded):
            nc.gpsimd.tensor_copy(
                dst[:].rearrange("p (t m) -> p t m", t=PACK), folded[:, 0, :].rearrange("p (m t) -> p t m", t=PACK)
            )

        def gather_half(dst, window, offsets, h):
            js = slice(h * J_HALF, (h + 1) * J_HALF)
            nc.vector.tensor_copy(dst[:, js], window[:].indirect(entries(offsets, h * J_HALF, J_HALF)))

        nc.vector.tensor_copy(xo_plane_picked[:], xo_plane[:].indirect(note_list[:]))
        unfold_plane(w2_folded)
        deal_plane(w2_plane_dealt, w2_folded)
        gather_half(xo_picked, xo_codes, note_list, 0)
        unfold_plane(w_folded)
        deal_plane(w_plane_dealt, w_folded)
        gather_half(xo_picked, xo_codes, note_list, 1)
        nc.vector.tensor_copy(xt_picked[:], xt_codes[:].indirect(token_list[:]))
        for h in range(HALVES):
            gather_half(xt_plane_picked, xt_plane, token_list, h)
        deal_words(w2_dealt, w2_codes, 2)
        deal_words(w_dealt, w_codes, 4)

        acc = [
            [psum.tile([P, J_HALF], F32, name=f"acc{h}_{t}", tag=f"bank{h}_{t}") for t in range(PACK)]
            for h in range(HALVES)
        ]
        g1 = [sbuf(f"g1_{t}", [P, J], F32) for t in range(PACK)]
        for h in range(HALVES):
            js = slice(h * J_HALF, (h + 1) * J_HALF)
            for t in range(PACK):
                rs = slice(t * P, (t + 1) * P)
                nc.tensor.matmul_mx(
                    acc[h][t][:], lhsT=w2_dealt[:, rs].bitcast(FP4X4), lhsT_scale=w2_plane_dealt[:, rs],
                    rhs=xo_picked[:, js].bitcast(FP8X4), rhs_scale=xo_plane_picked[:, js], start=True, stop=False,
                )
        for h in range(HALVES):
            js = slice(h * J_HALF, (h + 1) * J_HALF)
            for t in range(PACK):
                rs = slice(t * P, (t + 1) * P)
                nc.tensor.matmul_mx(
                    acc[h][t][:], lhsT=w_dealt[:, rs].bitcast(FP8X4), lhsT_scale=w_plane_dealt[:, rs],
                    rhs=xt_picked[:, js].bitcast(FP4X4), rhs_scale=xt_plane_picked[:, js], start=False, stop=True,
                )
                if h == 0 and t < PACK - 1:
                    nc.scalar.activation(g1[t][:, js], acc[h][t][:], ACT.Relu)
                else:
                    nc.vector.tensor_scalar_max(g1[t][:, js], acc[h][t][:], 0.0)

        hid = []
        for h in range(HALVES):
            hid.append(sbuf(f"hid{h}", [P, PACK, O_HALF], BF16, tag="hid0" if h == 0 else "sa0"))
            for t in range(PACK):
                nc.scalar.activation(
                    hid[h][:, t, :], g1[t][:].indirect(entries(slot_list, h * O_HALF, O_HALF)), ACT.Copy,
                    scale=sa_tiles[h][:, t : t + 1],
                )

        outcome_psum = [
            [psum.tile([P, O], F32, name=f"outcome_psum{k}_{nt}", tag=f"bank0_{2 * nt + k}") for k in range(2)]
            for nt in range(OUT_TILES)
        ]
        outcome = [[sbuf(f"outcome{k}_{nt}", [P, O], F32) for k in range(2)] for nt in range(OUT_TILES)]
        matrices = ((wb_codes, wb_plane, FP4X4), (wo_codes, wo_plane, FP8X4))
        for h in range(HALVES):
            places = slice(h * O_HALF, (h + 1) * O_HALF)
            woven = sbuf(f"woven{h}", [P, O_HALF, PACK], BF16, tag="woven0" if h == 0 else "hid_codes0")
            hid_codes = sbuf(f"hid_codes{h}", [P, O_HALF], U32)
            hid_plane = sbuf(f"hid_plane{h}", [P, O_HALF], U8)
            pieces = [slice(c, c + O_HALF // 2) for c in (0, O_HALF // 2)]
            for cs in pieces:
                nc.vector.tensor_copy(
                    woven[:, cs, :].rearrange("p (b i) t -> p b t i", i=PACK),
                    hid[h][:, :, cs].rearrange("p t (b i) -> p b t i", i=PACK),
                )
            for cs in pieces:
                nc.vector.quantize_mx(
                    out=hid_codes[:, cs].bitcast(FP8X4), scales=hid_plane[:, cs],
                    in_=woven[:, cs, :].rearrange("p c t -> p (c t)"),
                )
            for nt in range(OUT_TILES):
                ns = slice(nt * P, (nt + 1) * P)
                for k, (codes, plane, packed) in enumerate(matrices):
                    nc.tensor.matmul_mx(
                        outcome_psum[nt][k][:, places], lhsT=codes[:, ns].bitcast(packed), lhsT_scale=plane[:, ns],
                        rhs=hid_codes[:].bitcast(FP8X4), rhs_scale=hid_plane[:], start=True, stop=True,
                    )
                    nc.vector.tensor_copy(outcome[nt][k][:, places], outcome_psum[nt][k][:, places])

        page_order = [(nt, k) for nt in range(OUT_TILES) for k in range(2)]
        last_nt, last_k = page_order[-1]
        for h in range(HALVES):
            places = slice(h * O_HALF, (h + 1) * O_HALF)
            for nt, k in page_order[:-1]:
                nc.scalar.activation(
                    pages[nt][k][:].indirect(entries(put_lists[k], h * O_HALF, O_HALF)), outcome[nt][k][:, places],
                    ACT.Copy,
                )
        nc.scalar.activation(
            pages[last_nt][last_k][:].indirect(put_lists[last_k][:]), outcome[last_nt][last_k][:], ACT.Copy
        )

        larger = [sbuf(f"larger{nt}", [P, U], F32) for nt in range(OUT_TILES)]
        for nt in range(OUT_TILES):
            nc.vector.tensor_tensor(larger[nt][:], pages[nt][0][:], pages[nt][1][:], ALU.max)
        plus = [sbuf(f"plus{nt}", [P, E], F32) for nt in range(OUT_TILES)]
        minus = [sbuf(f"minus{nt}", [P, E], F32) for nt in range(OUT_TILES)]
        for nt in range(OUT_TILES):
            nc.scalar.activation(
                minus[nt][:], pages[nt][1][:].indirect(read_second[:]), ACT.Copy, scale=sf_tile[:, nt : nt + 1]
            )
            nc.scalar.activation(
                plus[nt][:], larger[nt][:].indirect(read_larger[:]), ACT.Copy, scale=se_tile[:, nt : nt + 1]
            )
            y = sbuf(f"y{nt}", [P, E], F32)
            nc.vector.tensor_tensor(y[:], plus[nt][:], minus[nt][:], ALU.subtract)
            nc.sync.dma_start(out[nt * P : (nt + 1) * P, :], y[:])
